import numpy as np
import ml_dtypes


def mxq(x, axis, fmt="e4m3"):
    dtype, down = {"e4m3": (ml_dtypes.float8_e4m3fn, 7), "e5m2": (ml_dtypes.float8_e5m2, 14)}[fmt]
    v = np.moveaxis(np.asarray(x, np.float32).astype(ml_dtypes.bfloat16).astype(np.float64), axis, -1)
    blocks = v.reshape(v.shape[:-1] + (-1, 32))
    amax = np.abs(blocks).max(-1, keepdims=True)
    byte = np.maximum(np.where(amax > 0, np.frexp(amax)[1] - 1 + 127, 0) - down, 1)
    scale = np.exp2(byte - 127.0)
    codes = (blocks / scale).astype(np.float32).astype(dtype).astype(np.float64)
    return np.moveaxis((codes * scale).reshape(v.shape), -1, axis)


WIDE = False


def mx_kscale(k):
    if not WIDE:
        return np.ones(k)
    levels = np.array([10, -10, 5, -5, 0])
    if k % 512:
        return np.exp2(np.random.permutation(np.resize(levels, k // 32))).repeat(32)
    a = np.empty((k // 512, 16))
    for p in range(k // 512):
        a[p, :8] = np.random.permutation(np.resize(levels, 8))
        for g in range(8):
            far = levels[np.abs(levels - a[p, g]) >= 10]
            a[p, g + 8] = far[np.random.randint(len(far))]
    return np.exp2(a.ravel()).repeat(32)


def f64(x):
    return np.asarray(x).astype(np.float64)


def striped(idx):
    return np.tile(np.asarray(idx).reshape(-1, 16).T, (8, 1)).astype(np.uint16)


def unstriped(offs):
    return offs[:16].T.reshape(-1).astype(np.int64)


E2M1 = np.array([0.0, 0.5, 1.0, 1.5, 2.0, 3.0, 4.0, 6.0, -0.0, -0.5, -1.0, -1.5, -2.0, -3.0, -4.0, -6.0])


def pack_weight(w, fmt):
    k, n = w.shape
    w = f64(np.asarray(w, np.float32).astype(ml_dtypes.bfloat16)).reshape(k // 32, 32, n)
    amax = np.abs(w).max(1)
    if fmt == "e4m3":
        byte = np.frexp(amax)[1] - 1 + 127 - 7
    else:
        mant, ex = np.frexp(amax / 6.0)
        byte = np.where(mant > 0.5, ex, ex - 1) + 127
    byte = np.clip(np.where(amax > 0, byte, 1), 1, 254)
    scaled = (w * np.exp2(127.0 - byte)[:, None, :]).reshape(k, n).astype(np.float32)
    by_word = np.ascontiguousarray(scaled.reshape(k // 512, 128, 4, n).transpose(0, 1, 3, 2))
    if fmt == "e4m3":
        words = by_word.astype(ml_dtypes.float8_e4m3fn).view(np.uint8)
    else:
        c = by_word.astype(ml_dtypes.float4_e2m1fn).view(np.uint8) & 0xF
        words = (c[..., 0::2] | (c[..., 1::2] << 4)).reshape(k // 512, 128, 2 * n)
    return np.ascontiguousarray(words), np.ascontiguousarray(byte.astype(np.uint8).reshape(k // 512, 16, n))


def unpack_weight(words, scales, fmt):
    g, _, n = scales.shape
    words = np.ascontiguousarray(words).reshape(g, 128, n, -1)
    if fmt == "e4m3":
        vals = words.view(ml_dtypes.float8_e4m3fn).astype(np.float64)
    else:
        nib = np.empty((g, 128, n, 4), np.uint8)
        nib[..., 0::2] = words & 0xF
        nib[..., 1::2] = words >> 4
        vals = E2M1[nib]
    vals = vals * np.repeat(np.exp2(scales.astype(np.float64) - 127.0), 8, axis=1)[..., None]
    return vals.transpose(0, 1, 3, 2).reshape(g * 512, n)


D, T, I, J, Q = 512, 4096, 512, 512, 128


def setup_inputs():
    n = np.random.standard_normal
    idx = np.random.permutation(T)[:I]
    idx2 = np.random.permutation(T)[:J]
    fd = mx_kscale(D)
    vocp = pack_weight(n((D, T)) / fd[:, None], "e2m1")
    return {
        "hid": (n((D, Q)) * 1.0 / np.sqrt(D) * fd[:, None]).astype(np.float32),
        "voc_words": vocp[0],
        "voc_scales": vocp[1],
        "lfreq": np.tile(np.random.uniform(-9.0, -5.0, T), (128, 1)).astype(np.float32),
        "tb": (np.random.uniform(-0.5, 0.5, (1, I))).astype(np.float32),
        "offs": striped(idx),
        "offs2": striped(idx2),
    }


def reference(hid, voc_words, voc_scales, lfreq, tb, offs, offs2):
    idx = unstriped(offs)
    idx2 = unstriped(offs2)
    vocu = unpack_weight(voc_words, voc_scales, "e2m1")
    hidq = mxq(f64(hid), 0, "e4m3")
    vocidxg = vocu[:, idx]
    a = hidq.T @ vocidxg
    vocidx2g = vocu[:, idx2]
    b = hidq.T @ vocidx2g
    r = b - f64(lfreq)[:1][:, idx2]
    m1 = np.max(r, axis=1, keepdims=True)
    z = np.log(np.sum(np.exp(r - m1), axis=1, keepdims=True)) + m1
    y = a + f64(tb) - z + 12.0
    return y

@@ -1,0 +1,149 @@
+import math
+from contextlib import ExitStack
+
+import concourse.mybir as mybir
+from concourse.masks import make_identity
+
+D, T, I, J, Q = 512, 4096, 512, 512, 128
+FLOPS = 2 * D * Q * (I + J)
+
+F32 = mybir.dt.float32
+BF16 = mybir.dt.bfloat16
+I32 = mybir.dt.int32
+U32 = mybir.dt.uint32
+U16 = mybir.dt.uint16
+U8 = mybir.dt.uint8
+FP8X4 = mybir.dt.float8_e4m3fn_x4
+FP4X4 = mybir.dt.float4_e2m1fn_x4
+ALU = mybir.AluOpType
+ACT = mybir.ActivationFunctionType
+P = 128
+PACK = 4
+ROW = P - 1
+TERMS = 10
+
+
+def tile_attend_sampledsum_kernel(tc, hid, voc_words, voc_scales, lfreq, tb, offs, offs2, out):
+    nc = tc.nc
+    with ExitStack() as ctx:
+        keep = ctx.enter_context(tc.tile_pool(name="keep", bufs=1))
+        psum = ctx.enter_context(tc.psum_pool(name="psum", bufs=1))
+
+        noise_list = keep.tile([P, J // 16], U16, name="noise_list")
+        target_list = keep.tile([P, I // 16], U16, name="target_list")
+        words = keep.tile([P, T], U16, name="words", align_bytes=64)
+        scales = keep.tile([P, T], U8, name="scales", align_bytes=64)
+        freq = keep.tile([P, T], F32, name="freq", align_bytes=64)
+        hid_raw = keep.tile([P, PACK, Q], F32, name="hid_raw", tag="staged", align_bytes=64)
+        ident = keep.tile([P, P], F32, name="ident", align_bytes=64)
+
+        nc.vector.memset(scales[:].bitcast(I32), 0)
+        nc.vector.memset(freq[0:ROW, :].bitcast(I32), 0)
+
+        nc.sync.dma_start(noise_list[:], offs2)
+        nc.sync.dma_start(freq[ROW:P, :], lfreq[0:1, :])
+        nc.sync.dma_start(hid_raw[:], hid.rearrange("(p t) q -> p t q", t=PACK))
+        nc.sync.dma_start(words[:].bitcast(I32), voc_words[0].bitcast(I32))
+        for quad in range(4):
+            nc.scalar.dma_start(
+                scales[32 * quad : 32 * quad + 4, :].bitcast(I32),
+                voc_scales[0, 4 * quad : 4 * quad + 4, :].bitcast(I32),
+            )
+        nc.sync.dma_start(target_list[:], offs)
+
+        make_identity(nc, ident[:])
+        factors = keep.tile([Q, 24], F32, name="factors", align_bytes=64)
+        addends = keep.tile([Q, 24], F32, name="addends", align_bytes=64)
+        for n in range(1, TERMS):
+            nc.gpsimd.memset(addends[:, 16 - n : 17 - n], (-1.0) ** n / n)
+        nc.gpsimd.memset(factors[:, 17:18], 1.0)
+
+        freq_row = keep.tile([P, J], F32, name="freq_row", align_bytes=64)
+        nc.vector.tensor_copy(freq_row[:], freq[:].indirect(noise_list[:]))
+        noise_scales = keep.tile([P, J], U8, name="noise_scales", align_bytes=64)
+        nc.vector.tensor_copy(noise_scales[:], scales[:].indirect(noise_list[:]))
+
+        hid_bf = keep.tile([P, Q, PACK], BF16, name="hid_bf", align_bytes=64)
+        nc.scalar.activation(hid_bf[:], hid_raw[:].rearrange("p t q -> p q t"), ACT.Copy)
+        tb_cols = keep.tile([P, PACK], F32, name="tb_cols", tag="staged", align_bytes=64)
+        nc.sync.dma_start(tb_cols[:], tb.rearrange("o (p c) -> (o p) c", c=PACK))
+        hid_codes = keep.tile([P, Q], U32, name="hid_codes", align_bytes=64)
+        hid_scales = keep.tile([P, Q], U8, name="hid_scales", align_bytes=64)
+        nc.vector.quantize_mx(
+            out=hid_codes[:].bitcast(FP8X4),
+            scales=hid_scales[:],
+            in_=hid_bf[:].rearrange("p q t -> p (q t)"),
+        )
+
+        turned = psum.tile([P, J // P, P], F32, name="turned")
+        for c in range(J // P):
+            nc.tensor.transpose(turned[:, c, :], freq_row[:, c * P : (c + 1) * P], ident[:])
+        freq_cols = keep.tile([P, J // P], F32, name="freq_cols")
+        nc.scalar.copy(freq_cols[:], turned[:, :, ROW])
+        freq_bank = psum.tile([P, J], F32, name="freq_bank")
+        for c in range(J // P):
+            nc.tensor.transpose(
+                freq_bank[:, c * P : (c + 1) * P], freq_cols[:, c : c + 1].to_broadcast([P, P]), ident[:]
+            )
+        freq_all = keep.tile([P, J], F32, name="freq_all", tag="late", align_bytes=64)
+        nc.scalar.copy(freq_all[:], freq_bank[:])
+
+        noise_words = keep.tile([P, J], U16, name="noise_words", align_bytes=64)
+        nc.vector.tensor_copy(noise_words[:], words[:].indirect(noise_list[:]))
+        noise_bank = psum.tile([Q, J], F32, name="noise_bank")
+        nc.tensor.matmul_mx(
+            out=noise_bank[:],
+            lhsT=hid_codes[:].bitcast(FP8X4),
+            lhsT_scale=hid_scales[:],
+            rhs=noise_words[:].bitcast(FP4X4),
+            rhs_scale=noise_scales[:],
+            start=True,
+            stop=True,
+        )
+        bias_bank = psum.tile([P, PACK, P], F32, name="bias_bank")
+        for c in range(PACK):
+            nc.tensor.transpose(bias_bank[:, c, :], tb_cols[:, c : c + 1].to_broadcast([P, P]), ident[:])
+        bias_all = keep.tile([Q, P, PACK], F32, name="bias_all", align_bytes=64)
+        nc.scalar.activation(bias_all[:], bias_bank[:].rearrange("q c n -> q n c"), ACT.Copy, bias=12.0)
+
+        target_scales = keep.tile([P, I], U8, name="target_scales", align_bytes=64)
+        nc.vector.tensor_copy(target_scales[:], scales[:].indirect(target_list[:]))
+
+        logits = keep.tile([Q, J], F32, name="logits", align_bytes=64)
+        nc.vector.tensor_tensor(logits[:], noise_bank[:], freq_all[:], ALU.subtract)
+        neg_max = addends[:, 17:18]
+        nc.vector.tensor_reduce(neg_max, logits[:], mybir.AxisListType.X, ALU.max, negate=True)
+        weights = keep.tile([Q, J], F32, name="weights", align_bytes=64)
+        total = keep.tile([Q, 1], F32, name="total")
+        nc.scalar.activation(weights[:], logits[:], ACT.Exp, bias=neg_max, scale=1.0, accum_out=total[:])
+        inverse = keep.tile([Q, 1], F32, name="inverse")
+        per_bit = math.log(2.0) / 2.0**23
+        nc.scalar.activation(inverse[:], total[:].bitcast(U32), ACT.Exp, bias=88.0, scale=-per_bit)
+        nc.scalar.activation(addends[:, 16:17], total[:].bitcast(U32), ACT.Identity, bias=88.0, scale=-per_bit)
+        nc.scalar.activation(
+            factors[:, 17 - TERMS : 17], inverse[:].to_broadcast([Q, TERMS]), ACT.Identity, bias=-1.0, scale=total[:]
+        )
+
+        target_words = keep.tile([P, I], U16, name="target_words", tag="late", align_bytes=64)
+        nc.vector.tensor_copy(target_words[:], words[:].indirect(target_list[:]))
+        target_bank = psum.tile([Q, I], F32, name="target_bank")
+        nc.tensor.matmul_mx(
+            out=target_bank[:],
+            lhsT=hid_codes[:].bitcast(FP8X4),
+            lhsT_scale=hid_scales[:],
+            rhs=target_words[:].bitcast(FP4X4),
+            rhs_scale=target_scales[:],
+            start=True,
+            stop=True,
+        )
+
+        horner = keep.tile([Q, TERMS + 1], F32, name="horner")
+        nc.vector.tensor_tensor_scan(
+            horner[:], factors[:, 17 - TERMS : 18], addends[:, 17 - TERMS : 18], (-1.0) ** TERMS / TERMS, ALU.mult, ALU.add
+        )
+        neg_z = horner[:, TERMS : TERMS + 1]
+        result = keep.tile([Q, I], F32, name="result", align_bytes=64)
+        nc.vector.scalar_tensor_tensor(
+            result[:], target_bank[:], neg_z, bias_all[:].rearrange("q n c -> q (n c)"), ALU.add, ALU.add
+        )
+        nc.sync.dma_start(out, result[:])

@@ -2,7 +2,6 @@ import math
 from contextlib import ExitStack
 
 import concourse.mybir as mybir
-from concourse.masks import make_identity
 
 D, T, I, J, Q = 512, 4096, 512, 512, 128
 FLOPS = 2 * D * Q * (I + J)
@@ -21,52 +20,52 @@ P = 128
 PACK = 4
 ROW = P - 1
 TERMS = 10
+HALF = 256
 
 
 def tile_attend_sampledsum_kernel(tc, hid, voc_words, voc_scales, lfreq, tb, offs, offs2, out):
     nc = tc.nc
     with ExitStack() as ctx:
         keep = ctx.enter_context(tc.tile_pool(name="keep", bufs=1))
+        loads = ctx.enter_context(tc.tile_pool(name="loads", bufs=1))
         psum = ctx.enter_context(tc.psum_pool(name="psum", bufs=1))
 
         noise_list = keep.tile([P, J // 16], U16, name="noise_list")
         target_list = keep.tile([P, I // 16], U16, name="target_list")
-        words = keep.tile([P, T], U16, name="words", align_bytes=64)
         scales = keep.tile([P, T], U8, name="scales", align_bytes=64)
-        freq = keep.tile([P, T], F32, name="freq", align_bytes=64)
-        hid_raw = keep.tile([P, PACK, Q], F32, name="hid_raw", tag="staged", align_bytes=64)
+        freq = keep.tile([P, T], F32, name="freq", tag="window", align_bytes=64)
+        diagonal = loads.tile([P, P], I32, name="diagonal", offset=2 * T - 256, align_bytes=64)
         ident = keep.tile([P, P], F32, name="ident", align_bytes=64)
+        hid_raw = keep.tile([P, PACK, Q], F32, name="hid_raw", align_bytes=64)
 
+        nc.gpsimd.iota(diagonal[:], pattern=[[-1, P]], base=0, channel_multiplier=1)
         nc.vector.memset(scales[:].bitcast(I32), 0)
+        nc.vector.tensor_scalar(ident[:], diagonal[:], 0.0, None, ALU.is_equal)
         nc.vector.memset(freq[0:ROW, :].bitcast(I32), 0)
 
         nc.sync.dma_start(noise_list[:], offs2)
         nc.sync.dma_start(freq[ROW:P, :], lfreq[0:1, :])
         nc.sync.dma_start(hid_raw[:], hid.rearrange("(p t) q -> p t q", t=PACK))
-        nc.sync.dma_start(words[:].bitcast(I32), voc_words[0].bitcast(I32))
-        for quad in range(4):
-            nc.scalar.dma_start(
-                scales[32 * quad : 32 * quad + 4, :].bitcast(I32),
-                voc_scales[0, 4 * quad : 4 * quad + 4, :].bitcast(I32),
-            )
         nc.sync.dma_start(target_list[:], offs)
-
-        make_identity(nc, ident[:])
-        factors = keep.tile([Q, 24], F32, name="factors", align_bytes=64)
-        addends = keep.tile([Q, 24], F32, name="addends", align_bytes=64)
-        for n in range(1, TERMS):
-            nc.gpsimd.memset(addends[:, 16 - n : 17 - n], (-1.0) ** n / n)
-        nc.gpsimd.memset(factors[:, 17:18], 1.0)
-
-        freq_row = keep.tile([P, J], F32, name="freq_row", align_bytes=64)
-        nc.vector.tensor_copy(freq_row[:], freq[:].indirect(noise_list[:]))
-        noise_scales = keep.tile([P, J], U8, name="noise_scales", align_bytes=64)
-        nc.vector.tensor_copy(noise_scales[:], scales[:].indirect(noise_list[:]))
+        for r in range(4):
+            nc.sync.dma_start(scales[r:P:32, :].bitcast(I32), voc_scales[0, r:16:4, :].bitcast(I32))
+        words = loads.tile([P, T], U16, name="words", offset=0, align_bytes=64)
+        nc.sync.dma_start(words[:].bitcast(I32), voc_words[0].bitcast(I32))
+        tb_cols = loads.tile([P, PACK], F32, name="tb_cols", offset=2 * T, align_bytes=64)
+        nc.sync.dma_start(tb_cols[:], tb.rearrange("o (p c) -> (o p) c", c=PACK))
 
         hid_bf = keep.tile([P, Q, PACK], BF16, name="hid_bf", align_bytes=64)
         nc.scalar.activation(hid_bf[:], hid_raw[:].rearrange("p t q -> p q t"), ACT.Copy)
-        tb_cols = keep.tile([P, PACK], F32, name="tb_cols", tag="staged", align_bytes=64)
-        nc.sync.dma_start(tb_cols[:], tb.rearrange("o (p c) -> (o p) c", c=PACK))
+
+        factors = keep.tile([Q, TERMS + 1], F32, name="factors")
+        addends = keep.tile([Q, TERMS + 1], F32, name="addends")
+        for n in range(1, TERMS):
+            col = TERMS - 1 - n
+            nc.scalar.activation(addends[:, col : col + 1], ident[:, 0:1], ACT.Copy, bias=(-1.0) ** n / n, scale=0.0)
+        nc.scalar.activation(factors[:, TERMS : TERMS + 1], ident[:, 0:1], ACT.Copy, bias=1.0, scale=0.0)
+
+        freq_row = keep.tile([P, J], F32, name="freq_row", align_bytes=64)
+        nc.vector.tensor_copy(freq_row[:], freq[:].indirect(noise_list[:]))
         hid_codes = keep.tile([P, Q], U32, name="hid_codes", align_bytes=64)
         hid_scales = keep.tile([P, Q], U8, name="hid_scales", align_bytes=64)
         nc.vector.quantize_mx(
@@ -75,7 +74,13 @@ def tile_attend_sampledsum_kernel(tc, hid, voc_words, voc_scales, lfreq, tb, off
             in_=hid_bf[:].rearrange("p q t -> p (q t)"),
         )
 
-        turned = psum.tile([P, J // P, P], F32, name="turned")
+        noise_scales = keep.tile([P, J], U8, name="noise_scales", tag="window", align_bytes=64)
+        nc.vector.tensor_copy(noise_scales[:], scales[:].indirect(noise_list[:]))
+
+        noise_words = keep.tile([P, J], U16, name="noise_words", align_bytes=64)
+        nc.vector.tensor_copy(noise_words[:], words[:].indirect(noise_list[:]))
+
+        turned = psum.tile([P, J // P, P], F32, name="turned", tag="turn")
         for c in range(J // P):
             nc.tensor.transpose(turned[:, c, :], freq_row[:, c * P : (c + 1) * P], ident[:])
         freq_cols = keep.tile([P, J // P], F32, name="freq_cols")
@@ -88,8 +93,6 @@ def tile_attend_sampledsum_kernel(tc, hid, voc_words, voc_scales, lfreq, tb, off
         freq_all = keep.tile([P, J], F32, name="freq_all", tag="late", align_bytes=64)
         nc.scalar.copy(freq_all[:], freq_bank[:])
 
-        noise_words = keep.tile([P, J], U16, name="noise_words", align_bytes=64)
-        nc.vector.tensor_copy(noise_words[:], words[:].indirect(noise_list[:]))
         noise_bank = psum.tile([Q, J], F32, name="noise_bank")
         nc.tensor.matmul_mx(
             out=noise_bank[:],
@@ -100,18 +103,18 @@ def tile_attend_sampledsum_kernel(tc, hid, voc_words, voc_scales, lfreq, tb, off
             start=True,
             stop=True,
         )
-        bias_bank = psum.tile([P, PACK, P], F32, name="bias_bank")
+        bias_bank = psum.tile([P, PACK, P], F32, name="bias_bank", tag="turn")
         for c in range(PACK):
             nc.tensor.transpose(bias_bank[:, c, :], tb_cols[:, c : c + 1].to_broadcast([P, P]), ident[:])
         bias_all = keep.tile([Q, P, PACK], F32, name="bias_all", align_bytes=64)
         nc.scalar.activation(bias_all[:], bias_bank[:].rearrange("q c n -> q n c"), ACT.Copy, bias=12.0)
 
-        target_scales = keep.tile([P, I], U8, name="target_scales", align_bytes=64)
-        nc.vector.tensor_copy(target_scales[:], scales[:].indirect(target_list[:]))
+        target_words = keep.tile([P, I], U16, name="target_words", align_bytes=64)
+        nc.vector.tensor_copy(target_words[:], words[:].indirect(target_list[:]))
 
         logits = keep.tile([Q, J], F32, name="logits", align_bytes=64)
         nc.vector.tensor_tensor(logits[:], noise_bank[:], freq_all[:], ALU.subtract)
-        neg_max = addends[:, 17:18]
+        neg_max = addends[:, TERMS : TERMS + 1]
         nc.vector.tensor_reduce(neg_max, logits[:], mybir.AxisListType.X, ALU.max, negate=True)
         weights = keep.tile([Q, J], F32, name="weights", align_bytes=64)
         total = keep.tile([Q, 1], F32, name="total")
@@ -119,31 +122,33 @@ def tile_attend_sampledsum_kernel(tc, hid, voc_words, voc_scales, lfreq, tb, off
         inverse = keep.tile([Q, 1], F32, name="inverse")
         per_bit = math.log(2.0) / 2.0**23
         nc.scalar.activation(inverse[:], total[:].bitcast(U32), ACT.Exp, bias=88.0, scale=-per_bit)
-        nc.scalar.activation(addends[:, 16:17], total[:].bitcast(U32), ACT.Identity, bias=88.0, scale=-per_bit)
+        nc.scalar.activation(addends[:, TERMS - 1 : TERMS], total[:].bitcast(U32), ACT.Identity, bias=88.0, scale=-per_bit)
         nc.scalar.activation(
-            factors[:, 17 - TERMS : 17], inverse[:].to_broadcast([Q, TERMS]), ACT.Identity, bias=-1.0, scale=total[:]
+            factors[:, 0:TERMS], inverse[:].to_broadcast([Q, TERMS]), ACT.Identity, bias=-1.0, scale=total[:]
         )
 
-        target_words = keep.tile([P, I], U16, name="target_words", tag="late", align_bytes=64)
-        nc.vector.tensor_copy(target_words[:], words[:].indirect(target_list[:]))
-        target_bank = psum.tile([Q, I], F32, name="target_bank")
-        nc.tensor.matmul_mx(
-            out=target_bank[:],
-            lhsT=hid_codes[:].bitcast(FP8X4),
-            lhsT_scale=hid_scales[:],
-            rhs=target_words[:].bitcast(FP4X4),
-            rhs_scale=target_scales[:],
-            start=True,
-            stop=True,
-        )
+        target_scales = keep.tile([P, I], U8, name="target_scales", tag="late", align_bytes=64)
+        nc.vector.tensor_copy(target_scales[:], scales[:].indirect(target_list[:]))
+        target_banks = [psum.tile([Q, HALF], F32, name="target_bank%d" % h) for h in range(2)]
+        for h in range(2):
+            nc.tensor.matmul_mx(
+                out=target_banks[h][:],
+                lhsT=hid_codes[:].bitcast(FP8X4),
+                lhsT_scale=hid_scales[:],
+                rhs=target_words[:, h * HALF : (h + 1) * HALF].bitcast(FP4X4),
+                rhs_scale=target_scales[:, h * HALF : (h + 1) * HALF],
+                start=True,
+                stop=True,
+            )
 
         horner = keep.tile([Q, TERMS + 1], F32, name="horner")
         nc.vector.tensor_tensor_scan(
-            horner[:], factors[:, 17 - TERMS : 18], addends[:, 17 - TERMS : 18], (-1.0) ** TERMS / TERMS, ALU.mult, ALU.add
+            horner[:], factors[:], addends[:], (-1.0) ** TERMS / TERMS, ALU.mult, ALU.add
         )
         neg_z = horner[:, TERMS : TERMS + 1]
-        result = keep.tile([Q, I], F32, name="result", align_bytes=64)
-        nc.vector.scalar_tensor_tensor(
-            result[:], target_bank[:], neg_z, bias_all[:].rearrange("q n c -> q (n c)"), ALU.add, ALU.add
-        )
-        nc.sync.dma_start(out, result[:])
+        bias_row = bias_all[:].rearrange("q n c -> q (n c)")
+        for h, queue in enumerate((nc.sync, nc.scalar)):
+            cols = slice(h * HALF, (h + 1) * HALF)
+            result = keep.tile([Q, HALF], F32, name="result%d" % h, align_bytes=64)
+            nc.vector.scalar_tensor_tensor(result[:], target_banks[h][:], neg_z, bias_row[:, cols], ALU.add, ALU.add)
+            queue.dma_start(out[:, cols], result[:])

@@ -20,7 +20,7 @@ P = 128
 PACK = 4
 ROW = P - 1
 TERMS = 10
-HALF = 256
+HALF = 128
 
 
 def tile_attend_sampledsum_kernel(tc, hid, voc_words, voc_scales, lfreq, tb, offs, offs2, out):
@@ -34,21 +34,30 @@ def tile_attend_sampledsum_kernel(tc, hid, voc_words, voc_scales, lfreq, tb, off
         target_list = keep.tile([P, I // 16], U16, name="target_list")
         scales = keep.tile([P, T], U8, name="scales", align_bytes=64)
         freq = keep.tile([P, T], F32, name="freq", tag="window", align_bytes=64)
-        diagonal = loads.tile([P, P], I32, name="diagonal", offset=2 * T - 256, align_bytes=64)
+        diagonal = keep.tile([P, P], I32, name="diagonal", align_bytes=64)
+        ones = loads.tile([P, 32], F32, name="ones", offset=2 * T - 64, align_bytes=64)
+        factors = keep.tile([Q, TERMS + 1], F32, name="factors")
+        addends = keep.tile([Q, TERMS + 1], F32, name="addends")
+        one = factors[:, TERMS : TERMS + 1]
         ident = keep.tile([P, P], F32, name="ident", align_bytes=64)
         hid_raw = keep.tile([P, PACK, Q], F32, name="hid_raw", align_bytes=64)
 
         nc.gpsimd.iota(diagonal[:], pattern=[[-1, P]], base=0, channel_multiplier=1)
         nc.vector.memset(scales[:].bitcast(I32), 0)
-        nc.vector.tensor_scalar(ident[:], diagonal[:], 0.0, None, ALU.is_equal)
+        nc.vector.memset(ones[:, 0:1], 1.0)
+        nc.scalar.copy(one, ones[:, 0:1])
         nc.vector.memset(freq[0:ROW, :].bitcast(I32), 0)
+        nc.vector.tensor_scalar(ident[:], diagonal[:], 0.0, None, ALU.is_equal)
 
         nc.sync.dma_start(noise_list[:], offs2)
         nc.sync.dma_start(freq[ROW:P, :], lfreq[0:1, :])
         nc.sync.dma_start(hid_raw[:], hid.rearrange("(p t) q -> p t q", t=PACK))
         nc.sync.dma_start(target_list[:], offs)
-        for r in range(4):
-            nc.sync.dma_start(scales[r:P:32, :].bitcast(I32), voc_scales[0, r:16:4, :].bitcast(I32))
+        for quad in (0, 2, 1, 3):
+            nc.sync.dma_start(
+                scales[32 * quad : 32 * quad + 4, :].bitcast(I32),
+                voc_scales[0, 4 * quad : 4 * quad + 4, :].bitcast(I32),
+            )
         words = loads.tile([P, T], U16, name="words", offset=0, align_bytes=64)
         nc.sync.dma_start(words[:].bitcast(I32), voc_words[0].bitcast(I32))
         tb_cols = loads.tile([P, PACK], F32, name="tb_cols", offset=2 * T, align_bytes=64)
@@ -57,12 +66,9 @@ def tile_attend_sampledsum_kernel(tc, hid, voc_words, voc_scales, lfreq, tb, off
         hid_bf = keep.tile([P, Q, PACK], BF16, name="hid_bf", align_bytes=64)
         nc.scalar.activation(hid_bf[:], hid_raw[:].rearrange("p t q -> p q t"), ACT.Copy)
 
-        factors = keep.tile([Q, TERMS + 1], F32, name="factors")
-        addends = keep.tile([Q, TERMS + 1], F32, name="addends")
         for n in range(1, TERMS):
             col = TERMS - 1 - n
-            nc.scalar.activation(addends[:, col : col + 1], ident[:, 0:1], ACT.Copy, bias=(-1.0) ** n / n, scale=0.0)
-        nc.scalar.activation(factors[:, TERMS : TERMS + 1], ident[:, 0:1], ACT.Copy, bias=1.0, scale=0.0)
+            nc.scalar.activation(addends[:, col : col + 1], one, ACT.Copy, scale=(-1.0) ** n / n)
 
         freq_row = keep.tile([P, J], F32, name="freq_row", align_bytes=64)
         nc.vector.tensor_copy(freq_row[:], freq[:].indirect(noise_list[:]))
@@ -129,8 +135,8 @@ def tile_attend_sampledsum_kernel(tc, hid, voc_words, voc_scales, lfreq, tb, off
 
         target_scales = keep.tile([P, I], U8, name="target_scales", tag="late", align_bytes=64)
         nc.vector.tensor_copy(target_scales[:], scales[:].indirect(target_list[:]))
-        target_banks = [psum.tile([Q, HALF], F32, name="target_bank%d" % h) for h in range(2)]
-        for h in range(2):
+        target_banks = [psum.tile([Q, HALF], F32, name="target_bank%d" % h) for h in range(I // HALF)]
+        for h in range(I // HALF):
             nc.tensor.matmul_mx(
                 out=target_banks[h][:],
                 lhsT=hid_codes[:].bitcast(FP8X4),
@@ -147,7 +153,7 @@ def tile_attend_sampledsum_kernel(tc, hid, voc_words, voc_scales, lfreq, tb, off
         )
         neg_z = horner[:, TERMS : TERMS + 1]
         bias_row = bias_all[:].rearrange("q n c -> q (n c)")
-        for h, queue in enumerate((nc.sync, nc.scalar)):
+        for h, queue in enumerate((nc.sync, nc.scalar, nc.sync, nc.scalar)):
             cols = slice(h * HALF, (h + 1) * HALF)
             result = keep.tile([Q, HALF], F32, name="result%d" % h, align_bytes=64)
             nc.vector.scalar_tensor_tensor(result[:], target_banks[h][:], neg_z, bias_row[:, cols], ALU.add, ALU.add)

import math
from contextlib import ExitStack

import concourse.mybir as mybir

D, T, I, J, Q = 512, 4096, 512, 512, 128
FLOPS = 2 * D * Q * (I + J)

F32 = mybir.dt.float32
BF16 = mybir.dt.bfloat16
I32 = mybir.dt.int32
U32 = mybir.dt.uint32
U16 = mybir.dt.uint16
U8 = mybir.dt.uint8
FP8X4 = mybir.dt.float8_e4m3fn_x4
FP4X4 = mybir.dt.float4_e2m1fn_x4
ALU = mybir.AluOpType
ACT = mybir.ActivationFunctionType
P = 128
PACK = 4
ROW = P - 1
TERMS = 10
HALF = 128


def tile_attend_sampledsum_kernel(tc, hid, voc_words, voc_scales, lfreq, tb, offs, offs2, out):
    nc = tc.nc
    with ExitStack() as ctx:
        keep = ctx.enter_context(tc.tile_pool(name="keep", bufs=1))
        loads = ctx.enter_context(tc.tile_pool(name="loads", bufs=1))
        psum = ctx.enter_context(tc.psum_pool(name="psum", bufs=1))

        noise_list = keep.tile([P, J // 16], U16, name="noise_list")
        target_list = keep.tile([P, I // 16], U16, name="target_list")
        scales = keep.tile([P, T], U8, name="scales", align_bytes=64)
        freq = keep.tile([P, T], F32, name="freq", tag="window", align_bytes=64)
        diagonal = keep.tile([P, P], I32, name="diagonal", align_bytes=64)
        ones = loads.tile([P, 32], F32, name="ones", offset=2 * T - 64, align_bytes=64)
        factors = keep.tile([Q, TERMS + 1], F32, name="factors")
        addends = keep.tile([Q, TERMS + 1], F32, name="addends")
        one = factors[:, TERMS : TERMS + 1]
        ident = keep.tile([P, P], F32, name="ident", align_bytes=64)
        hid_raw = keep.tile([P, PACK, Q], F32, name="hid_raw", align_bytes=64)

        nc.gpsimd.iota(diagonal[:], pattern=[[-1, P]], base=0, channel_multiplier=1)
        nc.vector.memset(scales[:].bitcast(I32), 0)
        nc.vector.memset(ones[:, 0:1], 1.0)
        nc.scalar.copy(one, ones[:, 0:1])
        nc.vector.memset(freq[0:ROW, :].bitcast(I32), 0)
        nc.vector.tensor_scalar(ident[:], diagonal[:], 0.0, None, ALU.is_equal)

        nc.sync.dma_start(noise_list[:], offs2)
        nc.sync.dma_start(freq[ROW:P, :], lfreq[0:1, :])
        nc.sync.dma_start(hid_raw[:], hid.rearrange("(p t) q -> p t q", t=PACK))
        nc.sync.dma_start(target_list[:], offs)
        for quad in (0, 2, 1, 3):
            nc.sync.dma_start(
                scales[32 * quad : 32 * quad + 4, :].bitcast(I32),
                voc_scales[0, 4 * quad : 4 * quad + 4, :].bitcast(I32),
            )
        words = loads.tile([P, T], U16, name="words", offset=0, align_bytes=64)
        nc.sync.dma_start(words[:].bitcast(I32), voc_words[0].bitcast(I32))
        tb_cols = loads.tile([P, PACK], F32, name="tb_cols", offset=2 * T, align_bytes=64)
        nc.sync.dma_start(tb_cols[:], tb.rearrange("o (p c) -> (o p) c", c=PACK))

        hid_bf = keep.tile([P, Q, PACK], BF16, name="hid_bf", align_bytes=64)
        nc.scalar.activation(hid_bf[:], hid_raw[:].rearrange("p t q -> p q t"), ACT.Copy)

        for n in range(1, TERMS):
            col = TERMS - 1 - n
            nc.scalar.activation(addends[:, col : col + 1], one, ACT.Copy, scale=(-1.0) ** n / n)

        freq_row = keep.tile([P, J], F32, name="freq_row", align_bytes=64)
        nc.vector.tensor_copy(freq_row[:], freq[:].indirect(noise_list[:]))
        hid_codes = keep.tile([P, Q], U32, name="hid_codes", align_bytes=64)
        hid_scales = keep.tile([P, Q], U8, name="hid_scales", align_bytes=64)
        nc.vector.quantize_mx(
            out=hid_codes[:].bitcast(FP8X4),
            scales=hid_scales[:],
            in_=hid_bf[:].rearrange("p q t -> p (q t)"),
        )

        noise_scales = keep.tile([P, J], U8, name="noise_scales", tag="window", align_bytes=64)
        nc.vector.tensor_copy(noise_scales[:], scales[:].indirect(noise_list[:]))

        noise_words = keep.tile([P, J], U16, name="noise_words", align_bytes=64)
        nc.vector.tensor_copy(noise_words[:], words[:].indirect(noise_list[:]))

        turned = psum.tile([P, J // P, P], F32, name="turned", tag="turn")
        for c in range(J // P):
            nc.tensor.transpose(turned[:, c, :], freq_row[:, c * P : (c + 1) * P], ident[:])
        freq_cols = keep.tile([P, J // P], F32, name="freq_cols")
        nc.scalar.copy(freq_cols[:], turned[:, :, ROW])
        freq_bank = psum.tile([P, J], F32, name="freq_bank")
        for c in range(J // P):
            nc.tensor.transpose(
                freq_bank[:, c * P : (c + 1) * P], freq_cols[:, c : c + 1].to_broadcast([P, P]), ident[:]
            )
        freq_all = keep.tile([P, J], F32, name="freq_all", tag="late", align_bytes=64)
        nc.scalar.copy(freq_all[:], freq_bank[:])

        noise_bank = psum.tile([Q, J], F32, name="noise_bank")
        nc.tensor.matmul_mx(
            out=noise_bank[:],
            lhsT=hid_codes[:].bitcast(FP8X4),
            lhsT_scale=hid_scales[:],
            rhs=noise_words[:].bitcast(FP4X4),
            rhs_scale=noise_scales[:],
            start=True,
            stop=True,
        )
        bias_bank = psum.tile([P, PACK, P], F32, name="bias_bank", tag="turn")
        for c in range(PACK):
            nc.tensor.transpose(bias_bank[:, c, :], tb_cols[:, c : c + 1].to_broadcast([P, P]), ident[:])
        bias_all = keep.tile([Q, P, PACK], F32, name="bias_all", align_bytes=64)
        nc.scalar.activation(bias_all[:], bias_bank[:].rearrange("q c n -> q n c"), ACT.Copy, bias=12.0)

        target_words = keep.tile([P, I], U16, name="target_words", align_bytes=64)
        nc.vector.tensor_copy(target_words[:], words[:].indirect(target_list[:]))

        logits = keep.tile([Q, J], F32, name="logits", align_bytes=64)
        nc.vector.tensor_tensor(logits[:], noise_bank[:], freq_all[:], ALU.subtract)
        neg_max = addends[:, TERMS : TERMS + 1]
        nc.vector.tensor_reduce(neg_max, logits[:], mybir.AxisListType.X, ALU.max, negate=True)
        weights = keep.tile([Q, J], F32, name="weights", align_bytes=64)
        total = keep.tile([Q, 1], F32, name="total")
        nc.scalar.activation(weights[:], logits[:], ACT.Exp, bias=neg_max, scale=1.0, accum_out=total[:])
        inverse = keep.tile([Q, 1], F32, name="inverse")
        per_bit = math.log(2.0) / 2.0**23
        nc.scalar.activation(inverse[:], total[:].bitcast(U32), ACT.Exp, bias=88.0, scale=-per_bit)
        nc.scalar.activation(addends[:, TERMS - 1 : TERMS], total[:].bitcast(U32), ACT.Identity, bias=88.0, scale=-per_bit)
        nc.scalar.activation(
            factors[:, 0:TERMS], inverse[:].to_broadcast([Q, TERMS]), ACT.Identity, bias=-1.0, scale=total[:]
        )

        target_scales = keep.tile([P, I], U8, name="target_scales", tag="late", align_bytes=64)
        nc.vector.tensor_copy(target_scales[:], scales[:].indirect(target_list[:]))
        target_banks = [psum.tile([Q, HALF], F32, name="target_bank%d" % h) for h in range(I // HALF)]
        for h in range(I // HALF):
            nc.tensor.matmul_mx(
                out=target_banks[h][:],
                lhsT=hid_codes[:].bitcast(FP8X4),
                lhsT_scale=hid_scales[:],
                rhs=target_words[:, h * HALF : (h + 1) * HALF].bitcast(FP4X4),
                rhs_scale=target_scales[:, h * HALF : (h + 1) * HALF],
                start=True,
                stop=True,
            )

        horner = keep.tile([Q, TERMS + 1], F32, name="horner")
        nc.vector.tensor_tensor_scan(
            horner[:], factors[:], addends[:], (-1.0) ** TERMS / TERMS, ALU.mult, ALU.add
        )
        neg_z = horner[:, TERMS : TERMS + 1]
        bias_row = bias_all[:].rearrange("q n c -> q (n c)")
        for h, queue in enumerate((nc.sync, nc.scalar, nc.sync, nc.scalar)):
            cols = slice(h * HALF, (h + 1) * HALF)
            result = keep.tile([Q, HALF], F32, name="result%d" % h, align_bytes=64)
            nc.vector.scalar_tensor_tensor(result[:], target_banks[h][:], neg_z, bias_row[:, cols], ALU.add, ALU.add)
            queue.dma_start(out[:, cols], result[:])
